import numpy as np
import ml_dtypes


def mxq(x, axis, fmt="e4m3"):
    dtype, down = {"e4m3": (ml_dtypes.float8_e4m3fn, 7), "e5m2": (ml_dtypes.float8_e5m2, 14)}[fmt]
    v = np.moveaxis(np.asarray(x, np.float32).astype(ml_dtypes.bfloat16).astype(np.float64), axis, -1)
    blocks = v.reshape(v.shape[:-1] + (-1, 32))
    amax = np.abs(blocks).max(-1, keepdims=True)
    byte = np.maximum(np.where(amax > 0, np.frexp(amax)[1] - 1 + 127, 0) - down, 1)
    scale = np.exp2(byte - 127.0)
    codes = (blocks / scale).astype(np.float32).astype(dtype).astype(np.float64)
    return np.moveaxis((codes * scale).reshape(v.shape), -1, axis)


WIDE = False


def mx_kscale(k):
    if not WIDE:
        return np.ones(k)
    levels = np.array([10, -10, 5, -5, 0])
    if k % 512:
        return np.exp2(np.random.permutation(np.resize(levels, k // 32))).repeat(32)
    a = np.empty((k // 512, 16))
    for p in range(k // 512):
        a[p, :8] = np.random.permutation(np.resize(levels, 8))
        for g in range(8):
            far = levels[np.abs(levels - a[p, g]) >= 10]
            a[p, g + 8] = far[np.random.randint(len(far))]
    return np.exp2(a.ravel()).repeat(32)


def f64(x):
    return np.asarray(x).astype(np.float64)


def striped(idx):
    return np.tile(idx.reshape(-1, 16).T, (8, 1)).astype(np.uint16)


def unstriped(offs):
    return offs[:16].T.reshape(-1).astype(np.int64)


def striped8(idx):
    return np.concatenate([x.reshape(-1, 16).T for x in idx]).astype(np.uint16)


def runs(offs, k):
    lists = np.stack([offs[16 * r : 16 * r + 16].T.reshape(-1) for r in range(8)]).astype(np.int64)
    return lists[np.arange(k) % 512 // 64]


def pack_weight(w):
    k, n = w.shape
    w = f64(np.asarray(w, np.float32).astype(ml_dtypes.bfloat16)).reshape(k // 32, 32, n)
    amax = np.abs(w).max(1)
    byte = np.clip(np.where(amax > 0, np.frexp(amax)[1] - 1 + 127 - 7, 1), 1, 254)
    scaled = (w * np.exp2(127.0 - byte)[:, None, :]).reshape(k, n).astype(np.float32)
    words = np.ascontiguousarray(scaled.reshape(k // 512, 128, 4, n).transpose(0, 1, 3, 2)).astype(ml_dtypes.float8_e4m3fn).view(np.uint8)
    return words, np.ascontiguousarray(byte.astype(np.uint8).reshape(k // 512, 16, n))


def unpack_weight(words, scales):
    g, p, n, _ = words.shape
    vals = np.ascontiguousarray(words).view(ml_dtypes.float8_e4m3fn).astype(np.float64) * np.repeat(np.exp2(scales.astype(np.float64) - 127.0), 8, axis=1)[..., None]
    return vals.transpose(0, 1, 3, 2).reshape(g * 512, n)


K, T, S, N, H = 512, 2048, 512, 512, 512


def setup_inputs():
    n = np.random.standard_normal
    s = mx_kscale(K)[:, None]
    u = mx_kscale(H)
    packed_xT = pack_weight(n((K, T)) * s)
    return {
        "x_words": packed_xT[0],
        "x_scales": packed_xT[1],
        "w1": (n((K, H)) / np.sqrt(K) / s).astype(np.float32),
        "gn": (np.random.uniform(0.5, 1.5, (H, 1)) * u[:, None]).astype(np.float32),
        "w2": (n((H, N)) / np.sqrt(H) / u[:, None]).astype(np.float32),
        "res": (2 * n((N, S))).astype(np.float32),
        "offs": striped(np.random.permutation(T)[:S]),
        "o1": striped8(np.stack([np.random.permutation(S) for _ in range(8)])),
        "o2": striped8(np.stack([np.random.permutation(S) for _ in range(8)])),
        "i1": striped8(np.stack([np.random.permutation(S) for _ in range(8)])),
        "i2": striped8(np.stack([np.random.permutation(S) for _ in range(8)])),
    }


def reference(x_words, x_scales, w1, gn, w2, res, offs, o1, o2, i1, i2):
    xq = unpack_weight(x_words, x_scales)[:, unstriped(offs)]
    y = mxq(f64(w1), 0, "e4m3").T @ xq
    hub = y[np.arange(H)[:, None], runs(o1, H)] + y[np.arange(H)[:, None], runs(o2, H)]
    hn = hub / (np.sqrt((hub) ** 2 + 1))
    z = f64(gn) * (hn[np.arange(H)[:, None], runs(i1, H)] + hn[np.arange(H)[:, None], runs(i2, H)])
    return f64(res) + (mxq(f64(w2), 0, "e4m3").T @ mxq(z, 0, "e4m3"))

@@ -1,0 +1,139 @@
+from contextlib import ExitStack
+
+import concourse.mybir as mybir
+
+K, T, S, N, H = 512, 2048, 512, 512, 512
+FLOPS = 2 * K * H * S + 2 * H * N * S
+
+F32 = mybir.dt.float32
+BF16 = mybir.dt.bfloat16
+I32 = mybir.dt.int32
+U32 = mybir.dt.uint32
+U16 = mybir.dt.uint16
+U8 = mybir.dt.uint8
+FP8X4 = mybir.dt.float8_e4m3fn_x4
+ACT = mybir.ActivationFunctionType
+ALU = mybir.AluOpType
+
+P = 128
+PACK = 4
+CHUNKS = ((0, 256), (256, 128), (384, 128))
+
+
+def tile_picked_hubauth_none_p_kernel(tc, x_words, x_scales, w1, gn, w2, res, offs, o1, o2, i1, i2, out):
+    nc = tc.nc
+    with ExitStack() as ctx:
+        keep = ctx.enter_context(tc.tile_pool(name="keep", bufs=1))
+        psum = ctx.enter_context(tc.psum_pool(name="psum", bufs=1))
+
+        def load_list(src, name):
+            t = keep.tile([P, S // 16], U16, name=name)
+            nc.sync.dma_start(t[:], src)
+            return t
+
+        xs = keep.tile([P, T], U8, name="xs", align_bytes=64)
+        nc.vector.memset(xs[:].bitcast(I32), 0)
+        offs_t = load_list(offs, "offs_t")
+        xw = keep.tile([P, T], I32, name="xw", align_bytes=64)
+        nc.sync.dma_start(xw[:], x_words[0].rearrange("p n t -> p (n t)").bitcast(I32))
+        for q in range(4):
+            nc.scalar.dma_start(xs[32 * q : 32 * q + 4, :].bitcast(I32), x_scales[0, 4 * q : 4 * q + 4, :].bitcast(I32))
+        w1raw = keep.tile([P, PACK, H], F32, name="w1raw")
+        nc.sync.dma_start(w1raw[:], w1.rearrange("(p j) c -> p j c", j=PACK))
+        o1_t = load_list(o1, "o1_t")
+        o2_t = load_list(o2, "o2_t")
+        gn_t = keep.tile([P, PACK], F32, name="gn_t")
+        nc.sync.dma_start(gn_t[:], gn.rearrange("(p t) o -> p (t o)", t=PACK))
+        w2raw = keep.tile([P, PACK, N], F32, name="w2raw")
+        nc.sync.dma_start(w2raw[:], w2.rearrange("(p j) c -> p j c", j=PACK))
+        i1_t = load_list(i1, "i1_t")
+        i2_t = load_list(i2, "i2_t")
+        res_t = keep.tile([P, N // P, S], F32, name="res_t")
+        nc.sync.dma_start(res_t[:], res.rearrange("(b p) c -> p b c", p=P))
+
+        ywin = [keep.tile([P, 2 * S], F32, name="ywin%d" % t) for t in range(PACK)]
+        for t in range(PACK):
+            nc.gpsimd.memset(ywin[t][:, S:], 0.0)
+
+        sg = keep.tile([P, S], U8, name="sg", align_bytes=64)
+        nc.vector.tensor_copy(sg[:], xs[:].indirect(offs_t[:]))
+        xg = keep.tile([P, S], U32, name="xg", align_bytes=64)
+        nc.vector.tensor_copy(xg[:], xw[:].bitcast(U32).indirect(offs_t[:]))
+
+        w1v = w1raw[:].rearrange("p j (m t) -> p m j t", t=PACK)
+        for h in range(2):
+            w1g = keep.tile([P, 2, P, PACK], BF16, name="w1g%d" % h, align_bytes=64)
+            nc.vector.tensor_copy(w1g[:].rearrange("p t m j -> p m j t"), w1v[:, :, :, 2 * h : 2 * h + 2])
+            w1c = keep.tile([P, 2 * P], U32, name="w1c%d" % h, align_bytes=64)
+            w1s = keep.tile([P, 2 * P], U8, name="w1s%d" % h, align_bytes=64)
+            nc.vector.quantize_mx(out=w1c[:].bitcast(FP8X4), scales=w1s[:], in_=w1g[:].rearrange("p t m j -> p (t m j)"))
+            for u in range(2):
+                t = 2 * h + u
+                yp = psum.tile([P, S], F32, name="yp%d" % t)
+                nc.tensor.matmul_mx(out=yp[:], lhsT=w1c[:, u * P : (u + 1) * P].bitcast(FP8X4), lhsT_scale=w1s[:, u * P : (u + 1) * P],
+                                    rhs=xg[:].bitcast(FP8X4), rhs_scale=sg[:], start=True, stop=True)
+                nc.scalar.copy(ywin[t][:, :S], yp[:])
+
+        hn = [keep.tile([P, S], F32, name="hn%d" % t) for t in range(PACK)]
+        hub = [keep.tile([P, S], F32, name="hub%d" % t) for t in range(PACK)]
+        rs = [keep.tile([P, S], F32, name="rs%d" % t) for t in range(PACK)]
+        w2g = keep.tile([P, N, PACK], BF16, name="w2g", align_bytes=64)
+        w2c = keep.tile([P, N], U32, name="w2c", align_bytes=64)
+        w2s = keep.tile([P, N], U8, name="w2s", align_bytes=64)
+
+        def normalise(t):
+            nc.vector.scalar_tensor_tensor(hn[t][:], hub[t][:], gn_t[:, t : t + 1], rs[t][:], ALU.mult, ALU.mult)
+
+        for h in range(2):
+            first = [keep.tile([P, S], F32, name="ga%d" % (2 * h + u)) for u in range(2)]
+            for u in range(2):
+                nc.vector.tensor_copy(first[u][:], ywin[2 * h + u][:].indirect(o1_t[:]))
+            for u in range(2):
+                t = 2 * h + u
+                nc.vector.tensor_tensor(hub[t][:], ywin[t][:].indirect(o2_t[:]), first[u][:], ALU.add)
+                sq = keep.tile([P, S], F32, name="sq%d" % t)
+                nc.scalar.activation(sq[:], hub[t][:], ACT.Square)
+                nc.scalar.activation(rs[t][:], sq[:], ACT.Abs_reciprocal_sqrt, bias=1.0)
+                if h == 1:
+                    normalise(u)
+            if h == 0:
+                for b in range(N // P):
+                    cols = slice(b * P, (b + 1) * P)
+                    nc.scalar.copy(w2g[:, cols, :].rearrange("p (c i) j -> p c j i", i=4), w2raw[:, :, cols].rearrange("p j (c i) -> p c j i", i=4))
+        nc.vector.quantize_mx(out=w2c[:].bitcast(FP8X4), scales=w2s[:], in_=w2g[:].rearrange("p c j -> p (c j)"))
+
+        outv = out.rearrange("(b p) c -> p b c", p=P)
+        for ci, (c0, cw) in enumerate(CHUNKS):
+            lc = slice(c0 // 16, (c0 + cw) // 16)
+            z = keep.tile([P, PACK, cw], F32, name="z%d" % ci)
+            for h in range(2):
+                first = [keep.tile([P, cw], F32, name="gb%d_%d" % (ci, 2 * h + u)) for u in range(2)]
+                if ci == 0 and h == 1:
+                    normalise(2)
+                    normalise(3)
+                for u in range(2):
+                    nc.vector.tensor_copy(first[u][:], hn[2 * h + u][:].indirect(i1_t[:, lc]))
+                for u in range(2):
+                    t = 2 * h + u
+                    nc.vector.tensor_tensor(z[:, t, :], hn[t][:].indirect(i2_t[:, lc]), first[u][:], ALU.add)
+            zg = keep.tile([P, cw, PACK], BF16, name="zg%d" % ci, align_bytes=64)
+            dst = zg[:].rearrange("p (c i) t -> p c t i", i=4)
+            src = z[:].rearrange("p t (c i) -> p c t i", i=4)
+            if ci == len(CHUNKS) - 1:
+                nc.vector.tensor_copy(dst, src)
+            else:
+                nc.scalar.copy(dst, src)
+            zc = keep.tile([P, cw], U32, name="zc%d" % ci, align_bytes=64)
+            zs = keep.tile([P, cw], U8, name="zs%d" % ci, align_bytes=64)
+            nc.vector.quantize_mx(out=zc[:].bitcast(FP8X4), scales=zs[:], in_=zg[:].rearrange("p c t -> p (c t)"))
+            per_bank = 512 // cw
+            for g in range(N // P // per_bank):
+                op = psum.tile([P, per_bank, cw], F32, name="op%d_%d" % (ci, g))
+                for u in range(per_bank):
+                    b = g * per_bank + u
+                    nc.tensor.matmul_mx(out=op[:, u, :], lhsT=w2c[:, b * P : (b + 1) * P].bitcast(FP8X4), lhsT_scale=w2s[:, b * P : (b + 1) * P],
+                                        rhs=zc[:].bitcast(FP8X4), rhs_scale=zs[:], start=True, stop=True)
+                blocks = slice(g * per_bank, (g + 1) * per_bank)
+                o_sb = keep.tile([P, per_bank, cw], F32, name="o%d_%d" % (ci, g))
+                nc.vector.tensor_tensor(o_sb[:], op[:], res_t[:, blocks, c0 : c0 + cw], ALU.add)
+                nc.sync.dma_start(outv[:, blocks, c0 : c0 + cw], o_sb[:])

@@ -1,6 +1,7 @@
 from contextlib import ExitStack
 
 import concourse.mybir as mybir
+from concourse.masks import make_identity
 
 K, T, S, N, H = 512, 2048, 512, 512, 512
 FLOPS = 2 * K * H * S + 2 * H * N * S
@@ -33,13 +34,13 @@ def tile_picked_hubauth_none_p_kernel(tc, x_words, x_scales, w1, gn, w2, res, of
 
         xs = keep.tile([P, T], U8, name="xs", align_bytes=64)
         nc.vector.memset(xs[:].bitcast(I32), 0)
+        w1raw = keep.tile([P, PACK, H], F32, name="w1raw")
+        nc.sync.dma_start(w1raw[:], w1.rearrange("(p j) c -> p j c", j=PACK))
+        for q in range(4):
+            nc.sync.dma_start(xs[32 * q : 32 * q + 4, :].bitcast(I32), x_scales[0, 4 * q : 4 * q + 4, :].bitcast(I32))
         offs_t = load_list(offs, "offs_t")
         xw = keep.tile([P, T], I32, name="xw", align_bytes=64)
         nc.sync.dma_start(xw[:], x_words[0].rearrange("p n t -> p (n t)").bitcast(I32))
-        for q in range(4):
-            nc.scalar.dma_start(xs[32 * q : 32 * q + 4, :].bitcast(I32), x_scales[0, 4 * q : 4 * q + 4, :].bitcast(I32))
-        w1raw = keep.tile([P, PACK, H], F32, name="w1raw")
-        nc.sync.dma_start(w1raw[:], w1.rearrange("(p j) c -> p j c", j=PACK))
         o1_t = load_list(o1, "o1_t")
         o2_t = load_list(o2, "o2_t")
         gn_t = keep.tile([P, PACK], F32, name="gn_t")
@@ -51,89 +52,158 @@ def tile_picked_hubauth_none_p_kernel(tc, x_words, x_scales, w1, gn, w2, res, of
         res_t = keep.tile([P, N // P, S], F32, name="res_t")
         nc.sync.dma_start(res_t[:], res.rearrange("(b p) c -> p b c", p=P))
 
+        warm = keep.tile([P, 2], F32, name="warm")
+        nc.gpsimd.memset(warm[:, 0:1], 0.0)
+        nc.scalar.activation(warm[:, 1:2], warm[:, 0:1], ACT.Abs_reciprocal_sqrt, bias=1.0)
+        ident = keep.tile([P, P], F32, name="ident")
+        make_identity(nc, ident[:])
         ywin = [keep.tile([P, 2 * S], F32, name="ywin%d" % t) for t in range(PACK)]
         for t in range(PACK):
-            nc.gpsimd.memset(ywin[t][:, S:], 0.0)
-
-        sg = keep.tile([P, S], U8, name="sg", align_bytes=64)
-        nc.vector.tensor_copy(sg[:], xs[:].indirect(offs_t[:]))
-        xg = keep.tile([P, S], U32, name="xg", align_bytes=64)
-        nc.vector.tensor_copy(xg[:], xw[:].bitcast(U32).indirect(offs_t[:]))
+            nc.vector.memset(ywin[t][:, S:], 0.0)
 
         w1v = w1raw[:].rearrange("p j (m t) -> p m j t", t=PACK)
-        for h in range(2):
-            w1g = keep.tile([P, 2, P, PACK], BF16, name="w1g%d" % h, align_bytes=64)
-            nc.vector.tensor_copy(w1g[:].rearrange("p t m j -> p m j t"), w1v[:, :, :, 2 * h : 2 * h + 2])
-            w1c = keep.tile([P, 2 * P], U32, name="w1c%d" % h, align_bytes=64)
-            w1s = keep.tile([P, 2 * P], U8, name="w1s%d" % h, align_bytes=64)
-            nc.vector.quantize_mx(out=w1c[:].bitcast(FP8X4), scales=w1s[:], in_=w1g[:].rearrange("p t m j -> p (t m j)"))
-            for u in range(2):
-                t = 2 * h + u
-                yp = psum.tile([P, S], F32, name="yp%d" % t)
-                nc.tensor.matmul_mx(out=yp[:], lhsT=w1c[:, u * P : (u + 1) * P].bitcast(FP8X4), lhsT_scale=w1s[:, u * P : (u + 1) * P],
-                                    rhs=xg[:].bitcast(FP8X4), rhs_scale=sg[:], start=True, stop=True)
-                nc.scalar.copy(ywin[t][:, :S], yp[:])
+        w1g = [keep.tile([P, 2, P, PACK], BF16, name="w1g%d" % h, align_bytes=64) for h in range(2)]
+        w1c = [keep.tile([P, 2 * P], U32, name="w1c%d" % h, align_bytes=64) for h in range(2)]
+        w1s = [keep.tile([P, 2 * P], U8, name="w1s%d" % h, align_bytes=64) for h in range(2)]
+        sg = keep.tile([P, S], U8, name="sg", align_bytes=64)
+        nc.vector.tensor_copy(w1g[0][:].rearrange("p t m j -> p m j t"), w1v[:, :, :, 0:2])
+        nc.scalar.copy(w1g[1][:].rearrange("p t m j -> p m j t"), w1v[:, :, :, 2:4])
+        nc.vector.tensor_copy(sg[:], xs[:].indirect(offs_t[:]))
 
-        hn = [keep.tile([P, S], F32, name="hn%d" % t) for t in range(PACK)]
+        def quantise_w1(h):
+            nc.vector.quantize_mx(out=w1c[h][:].bitcast(FP8X4), scales=w1s[h][:], in_=w1g[h][:].rearrange("p t m j -> p (t m j)"))
+
+        quantise_w1(0)
+
+        xg = keep.tile([P, S], U32, name="xg", align_bytes=64)
+        half = S // 2
+        for a in range(2):
+            nc.vector.tensor_copy(xg[:, a * half : (a + 1) * half], xw[:].bitcast(U32).indirect(offs_t[:, a * half // 16 : (a + 1) * half // 16]))
+
+        def project(t, cols, evacuate):
+            h, u = divmod(t, 2)
+            yp = psum.tile([P, cols.stop - cols.start], F32, name="yp%d_%d" % (t, cols.start), tag="bank", bufs=8)
+            nc.tensor.matmul_mx(out=yp[:], lhsT=w1c[h][:, u * P : (u + 1) * P].bitcast(FP8X4), lhsT_scale=w1s[h][:, u * P : (u + 1) * P],
+                                rhs=xg[:, cols].bitcast(FP8X4), rhs_scale=sg[:, cols], start=True, stop=True)
+            evacuate(ywin[t][:, cols], yp[:])
+
+        quantise_w1(1)
+        project(0, slice(0, half), nc.scalar.copy)
+        project(1, slice(0, half), nc.scalar.copy)
+        project(0, slice(half, S), nc.vector.tensor_copy)
+        project(1, slice(half, S), nc.scalar.copy)
+        for t in range(2, PACK):
+            project(t, slice(0, S), nc.scalar.copy)
+
+        ga = [keep.tile([P, S], F32, name="ga%d" % t) for t in range(PACK)]
+        hn = [ga[1], ga[3], keep.tile([P, S], F32, name="hn2"), keep.tile([P, S], F32, name="hn3")]
         hub = [keep.tile([P, S], F32, name="hub%d" % t) for t in range(PACK)]
-        rs = [keep.tile([P, S], F32, name="rs%d" % t) for t in range(PACK)]
-        w2g = keep.tile([P, N, PACK], BF16, name="w2g", align_bytes=64)
+        zb = keep.tile([P, S], F32, name="zb")
+        rs = [keep.tile([P, S], F32, name="rs%d" % t)[:] for t in range(PACK - 1)] + [zb[:]]
+        w2buf = keep.tile([P, 3 * S + 256], F32, name="w2buf", align_bytes=64)
+        w2g = w2buf[:, : 2 * S].bitcast(BF16).rearrange("p (c j) -> p c j", j=PACK)
+        gained = [keep.tile([P, S], F32, name="gained%d" % t)[:] for t in range(PACK - 1)] + [w2buf[:, 768:1280]]
         w2c = keep.tile([P, N], U32, name="w2c", align_bytes=64)
         w2s = keep.tile([P, N], U8, name="w2s", align_bytes=64)
 
         def normalise(t):
-            nc.vector.scalar_tensor_tensor(hn[t][:], hub[t][:], gn_t[:, t : t + 1], rs[t][:], ALU.mult, ALU.mult)
+            nc.gpsimd.tensor_tensor(hn[t][:], gained[t], rs[t], ALU.mult)
+
+        def fetch_first(t):
+            nc.vector.tensor_copy(ga[t][:], ywin[t][:].indirect(o1_t[:]))
+
+        def add_second(t):
+            nc.vector.tensor_tensor(hub[t][:], ywin[t][:].indirect(o2_t[:]), ga[t][:], ALU.add)
+            sq = keep.tile([P, S], F32, name="sq%d" % t)
+            nc.scalar.activation(sq[:], hub[t][:], ACT.Square)
+            nc.scalar.activation(rs[t], sq[:], ACT.Abs_reciprocal_sqrt, bias=1.0)
+            nc.scalar.activation(gained[t], hub[t][:], ACT.Copy, scale=gn_t[:, t : t + 1])
+
+        def weave_w2(b):
+            cols = slice(b * P, (b + 1) * P)
+            nc.scalar.copy(w2g[:, cols, :].rearrange("p (c i) j -> p c j i", i=4), w2raw[:, :, cols].rearrange("p j (c i) -> p c j i", i=4))
 
         for h in range(2):
-            first = [keep.tile([P, S], F32, name="ga%d" % (2 * h + u)) for u in range(2)]
-            for u in range(2):
-                nc.vector.tensor_copy(first[u][:], ywin[2 * h + u][:].indirect(o1_t[:]))
-            for u in range(2):
-                t = 2 * h + u
-                nc.vector.tensor_tensor(hub[t][:], ywin[t][:].indirect(o2_t[:]), first[u][:], ALU.add)
-                sq = keep.tile([P, S], F32, name="sq%d" % t)
-                nc.scalar.activation(sq[:], hub[t][:], ACT.Square)
-                nc.scalar.activation(rs[t][:], sq[:], ACT.Abs_reciprocal_sqrt, bias=1.0)
-                if h == 1:
-                    normalise(u)
-            if h == 0:
-                for b in range(N // P):
-                    cols = slice(b * P, (b + 1) * P)
-                    nc.scalar.copy(w2g[:, cols, :].rearrange("p (c i) j -> p c j i", i=4), w2raw[:, :, cols].rearrange("p j (c i) -> p c j i", i=4))
-        nc.vector.quantize_mx(out=w2c[:].bitcast(FP8X4), scales=w2s[:], in_=w2g[:].rearrange("p c j -> p (c j)"))
+            fetch_first(2 * h)
+            fetch_first(2 * h + 1)
+            add_second(2 * h)
+            add_second(2 * h + 1)
+            normalise(h)
+        normalise(2)
+        normalise(3)
+        for b in range(N // P):
+            weave_w2(b)
 
         outv = out.rearrange("(b p) c -> p b c", p=P)
-        for ci, (c0, cw) in enumerate(CHUNKS):
-            lc = slice(c0 // 16, (c0 + cw) // 16)
-            z = keep.tile([P, PACK, cw], F32, name="z%d" % ci)
-            for h in range(2):
-                first = [keep.tile([P, cw], F32, name="gb%d_%d" % (ci, 2 * h + u)) for u in range(2)]
-                if ci == 0 and h == 1:
-                    normalise(2)
-                    normalise(3)
-                for u in range(2):
-                    nc.vector.tensor_copy(first[u][:], hn[2 * h + u][:].indirect(i1_t[:, lc]))
-                for u in range(2):
-                    t = 2 * h + u
-                    nc.vector.tensor_tensor(z[:, t, :], hn[t][:].indirect(i2_t[:, lc]), first[u][:], ALU.add)
-            zg = keep.tile([P, cw, PACK], BF16, name="zg%d" % ci, align_bytes=64)
-            dst = zg[:].rearrange("p (c i) t -> p c t i", i=4)
-            src = z[:].rearrange("p t (c i) -> p c t i", i=4)
-            if ci == len(CHUNKS) - 1:
-                nc.vector.tensor_copy(dst, src)
-            else:
-                nc.scalar.copy(dst, src)
-            zc = keep.tile([P, cw], U32, name="zc%d" % ci, align_bytes=64)
-            zs = keep.tile([P, cw], U8, name="zs%d" % ci, align_bytes=64)
-            nc.vector.quantize_mx(out=zc[:].bitcast(FP8X4), scales=zs[:], in_=zg[:].rearrange("p c t -> p (c t)"))
-            per_bank = 512 // cw
-            for g in range(N // P // per_bank):
-                op = psum.tile([P, per_bank, cw], F32, name="op%d_%d" % (ci, g))
+        wide = 2 * P
+        left = [keep.tile([P, wide], F32, name="left%d" % t) for t in range(PACK)]
+        left2 = [keep.tile([P, wide], F32, name="leftb%d" % t) for t in range(PACK)]
+        right = [keep.tile([P, wide], F32, name="right%d" % t) for t in range(PACK)]
+        zlast = w2buf[:, 2 * S : 3 * S]
+        woven01_words = w2buf[:, 2 * S + wide : 3 * S + wide]
+        late = keep.tile([P, S], F32, name="late", align_bytes=64)
+        woven3 = late[:, :wide].bitcast(BF16)
+        woven01 = woven01_words.bitcast(BF16)
+        woven2 = w2buf[:, 2 * S + 3 * P : 2 * S + 5 * P].bitcast(BF16)
+        zt = [psum.tile([P, PACK, P], F32, name="zt%d" % jb, tag="bank", bufs=8) for jb in range(2)]
+
+        def fetch(dst, t, lst, lo, hi):
+            nc.vector.tensor_copy(dst[:], hn[t][:].indirect(lst[:, lo // 16 : hi // 16]))
+
+        def second(z, jb, t):
+            lc = slice(jb * P // 16, (jb + 1) * P // 16)
+            nc.vector.tensor_tensor(z[:, t * P : (t + 1) * P], hn[t][:].indirect(i2_t[:, lc]), right[t][:, (jb - 2) * P : (jb - 1) * P], ALU.add)
+
+        def weave(dst, z, copy):
+            copy(dst.rearrange("p (c i t) -> p c t i", i=4, t=PACK), z.rearrange("p (t c i) -> p c t i", t=PACK, i=4))
+
+        def quantise(woven, width, name):
+            codes = keep.tile([P, width], U32, name="zcodes" + name, align_bytes=64)
+            scales = keep.tile([P, width], U8, name="zscales" + name, align_bytes=64)
+            nc.vector.quantize_mx(out=codes[:].bitcast(FP8X4), scales=scales[:], in_=woven)
+            return codes, scales
+
+        def finish(lo, width, codes, scales, per_bank, queues, staged=None):
+            cols = slice(lo, lo + width)
+            for g, queue in enumerate(queues):
+                op = psum.tile([P, per_bank, width], F32, name="op%d_%d" % (lo, g), tag="bank", bufs=8)
                 for u in range(per_bank):
                     b = g * per_bank + u
                     nc.tensor.matmul_mx(out=op[:, u, :], lhsT=w2c[:, b * P : (b + 1) * P].bitcast(FP8X4), lhsT_scale=w2s[:, b * P : (b + 1) * P],
-                                        rhs=zc[:].bitcast(FP8X4), rhs_scale=zs[:], start=True, stop=True)
+                                        rhs=codes[:].bitcast(FP8X4), rhs_scale=scales[:], start=True, stop=True)
                 blocks = slice(g * per_bank, (g + 1) * per_bank)
-                o_sb = keep.tile([P, per_bank, cw], F32, name="o%d_%d" % (ci, g))
-                nc.vector.tensor_tensor(o_sb[:], op[:], res_t[:, blocks, c0 : c0 + cw], ALU.add)
-                nc.sync.dma_start(outv[:, blocks, c0 : c0 + cw], o_sb[:])
+                o_sb = staged if staged is not None else keep.tile([P, per_bank, width], F32, name="o%d_%d" % (lo, g))[:]
+                nc.vector.tensor_tensor(o_sb, op[:], res_t[:, blocks, cols], ALU.add)
+                queue.dma_start(outv[:, blocks, cols], o_sb)
+
+        for t in range(PACK):
+            fetch(left[t], t, i1_t, 0, wide)
+            fetch(left2[t], t, i2_t, 0, wide)
+            for jb in range(2):
+                cols = slice(jb * P, (jb + 1) * P)
+                nc.tensor.matmul(zt[jb][:, t, :], left[t][:, cols], ident[:], start=True, stop=False, is_transpose=True)
+                nc.tensor.matmul(zt[jb][:, t, :], left2[t][:, cols], ident[:], start=False, stop=True, is_transpose=True)
+            fetch(right[t], t, i1_t, wide, S)
+        for jb in range(2):
+            pairs = keep.tile([P, 2, P, 2], BF16, name="pairs%d" % jb)
+            nc.scalar.copy(pairs[:], zt[jb][:].rearrange("j (u e) p -> j u p e", e=2))
+            words = pairs[:].rearrange("j u p e -> j (u p e)").bitcast(F32)
+            back = psum.tile([P, 2, P], F32, name="back%d" % jb, tag="bank", bufs=8)
+            for u in range(2):
+                nc.tensor.transpose(back[:, u, :], words[:, u * P : (u + 1) * P], ident[:])
+            nc.scalar.copy(woven01_words[:, jb * wide : (jb + 1) * wide].rearrange("p (c u) -> p c u", u=2), back[:].rearrange("p u c -> p c u"))
+        nc.vector.quantize_mx(out=w2c[:].bitcast(FP8X4), scales=w2s[:], in_=w2g.rearrange("p c j -> p (c j)"))
+        for t in range(PACK):
+            second(zb, 2, t)
+        second(zlast, 3, 0)
+        second(zlast, 3, 1)
+        q01 = quantise(woven01, wide, "01")
+        weave(woven2, zb[:], nc.scalar.copy)
+        second(zlast, 3, 2)
+        finish(0, wide, *q01, 2, [nc.sync, nc.sync])
+        q2 = quantise(woven2, P, "2")
+        second(zlast, 3, PACK - 1)
+        weave(woven3, zlast, nc.vector.tensor_copy)
+        q3 = quantise(woven3, P, "3")
+        finish(2 * P, P, *q2, 4, [nc.sync], late[:].rearrange("p (b c) -> p b c", c=P))
+        finish(3 * P, P, *q3, 2, [nc.sync, nc.scalar])

from contextlib import ExitStack

import concourse.mybir as mybir
from concourse.masks import make_identity

K, T, S, N, H = 512, 2048, 512, 512, 512
FLOPS = 2 * K * H * S + 2 * H * N * S

F32 = mybir.dt.float32
BF16 = mybir.dt.bfloat16
I32 = mybir.dt.int32
U32 = mybir.dt.uint32
U16 = mybir.dt.uint16
U8 = mybir.dt.uint8
FP8X4 = mybir.dt.float8_e4m3fn_x4
ACT = mybir.ActivationFunctionType
ALU = mybir.AluOpType

P = 128
PACK = 4
CHUNKS = ((0, 256), (256, 128), (384, 128))


def tile_picked_hubauth_none_p_kernel(tc, x_words, x_scales, w1, gn, w2, res, offs, o1, o2, i1, i2, out):
    nc = tc.nc
    with ExitStack() as ctx:
        keep = ctx.enter_context(tc.tile_pool(name="keep", bufs=1))
        psum = ctx.enter_context(tc.psum_pool(name="psum", bufs=1))

        def load_list(src, name):
            t = keep.tile([P, S // 16], U16, name=name)
            nc.sync.dma_start(t[:], src)
            return t

        xs = keep.tile([P, T], U8, name="xs", align_bytes=64)
        nc.vector.memset(xs[:].bitcast(I32), 0)
        w1raw = keep.tile([P, PACK, H], F32, name="w1raw")
        nc.sync.dma_start(w1raw[:], w1.rearrange("(p j) c -> p j c", j=PACK))
        for q in range(4):
            nc.sync.dma_start(xs[32 * q : 32 * q + 4, :].bitcast(I32), x_scales[0, 4 * q : 4 * q + 4, :].bitcast(I32))
        offs_t = load_list(offs, "offs_t")
        xw = keep.tile([P, T], I32, name="xw", align_bytes=64)
        nc.sync.dma_start(xw[:], x_words[0].rearrange("p n t -> p (n t)").bitcast(I32))
        o1_t = load_list(o1, "o1_t")
        o2_t = load_list(o2, "o2_t")
        gn_t = keep.tile([P, PACK], F32, name="gn_t")
        nc.sync.dma_start(gn_t[:], gn.rearrange("(p t) o -> p (t o)", t=PACK))
        w2raw = keep.tile([P, PACK, N], F32, name="w2raw")
        nc.sync.dma_start(w2raw[:], w2.rearrange("(p j) c -> p j c", j=PACK))
        i1_t = load_list(i1, "i1_t")
        i2_t = load_list(i2, "i2_t")
        res_t = keep.tile([P, N // P, S], F32, name="res_t")
        nc.sync.dma_start(res_t[:], res.rearrange("(b p) c -> p b c", p=P))

        warm = keep.tile([P, 2], F32, name="warm")
        nc.gpsimd.memset(warm[:, 0:1], 0.0)
        nc.scalar.activation(warm[:, 1:2], warm[:, 0:1], ACT.Abs_reciprocal_sqrt, bias=1.0)
        ident = keep.tile([P, P], F32, name="ident")
        make_identity(nc, ident[:])
        ywin = [keep.tile([P, 2 * S], F32, name="ywin%d" % t) for t in range(PACK)]
        for t in range(PACK):
            nc.vector.memset(ywin[t][:, S:], 0.0)

        w1v = w1raw[:].rearrange("p j (m t) -> p m j t", t=PACK)
        w1g = [keep.tile([P, 2, P, PACK], BF16, name="w1g%d" % h, align_bytes=64) for h in range(2)]
        w1c = [keep.tile([P, 2 * P], U32, name="w1c%d" % h, align_bytes=64) for h in range(2)]
        w1s = [keep.tile([P, 2 * P], U8, name="w1s%d" % h, align_bytes=64) for h in range(2)]
        sg = keep.tile([P, S], U8, name="sg", align_bytes=64)
        nc.vector.tensor_copy(w1g[0][:].rearrange("p t m j -> p m j t"), w1v[:, :, :, 0:2])
        nc.scalar.copy(w1g[1][:].rearrange("p t m j -> p m j t"), w1v[:, :, :, 2:4])
        nc.vector.tensor_copy(sg[:], xs[:].indirect(offs_t[:]))

        def quantise_w1(h):
            nc.vector.quantize_mx(out=w1c[h][:].bitcast(FP8X4), scales=w1s[h][:], in_=w1g[h][:].rearrange("p t m j -> p (t m j)"))

        quantise_w1(0)

        xg = keep.tile([P, S], U32, name="xg", align_bytes=64)
        half = S // 2
        for a in range(2):
            nc.vector.tensor_copy(xg[:, a * half : (a + 1) * half], xw[:].bitcast(U32).indirect(offs_t[:, a * half // 16 : (a + 1) * half // 16]))

        def project(t, cols, evacuate):
            h, u = divmod(t, 2)
            yp = psum.tile([P, cols.stop - cols.start], F32, name="yp%d_%d" % (t, cols.start), tag="bank", bufs=8)
            nc.tensor.matmul_mx(out=yp[:], lhsT=w1c[h][:, u * P : (u + 1) * P].bitcast(FP8X4), lhsT_scale=w1s[h][:, u * P : (u + 1) * P],
                                rhs=xg[:, cols].bitcast(FP8X4), rhs_scale=sg[:, cols], start=True, stop=True)
            evacuate(ywin[t][:, cols], yp[:])

        quantise_w1(1)
        project(0, slice(0, half), nc.scalar.copy)
        project(1, slice(0, half), nc.scalar.copy)
        project(0, slice(half, S), nc.vector.tensor_copy)
        project(1, slice(half, S), nc.scalar.copy)
        for t in range(2, PACK):
            project(t, slice(0, S), nc.scalar.copy)

        ga = [keep.tile([P, S], F32, name="ga%d" % t) for t in range(PACK)]
        hn = [ga[1], ga[3], keep.tile([P, S], F32, name="hn2"), keep.tile([P, S], F32, name="hn3")]
        hub = [keep.tile([P, S], F32, name="hub%d" % t) for t in range(PACK)]
        zb = keep.tile([P, S], F32, name="zb")
        rs = [keep.tile([P, S], F32, name="rs%d" % t)[:] for t in range(PACK - 1)] + [zb[:]]
        w2buf = keep.tile([P, 3 * S + 256], F32, name="w2buf", align_bytes=64)
        w2g = w2buf[:, : 2 * S].bitcast(BF16).rearrange("p (c j) -> p c j", j=PACK)
        gained = [keep.tile([P, S], F32, name="gained%d" % t)[:] for t in range(PACK - 1)] + [w2buf[:, 768:1280]]
        w2c = keep.tile([P, N], U32, name="w2c", align_bytes=64)
        w2s = keep.tile([P, N], U8, name="w2s", align_bytes=64)

        def normalise(t):
            nc.gpsimd.tensor_tensor(hn[t][:], gained[t], rs[t], ALU.mult)

        def fetch_first(t):
            nc.vector.tensor_copy(ga[t][:], ywin[t][:].indirect(o1_t[:]))

        def add_second(t):
            nc.vector.tensor_tensor(hub[t][:], ywin[t][:].indirect(o2_t[:]), ga[t][:], ALU.add)
            sq = keep.tile([P, S], F32, name="sq%d" % t)
            nc.scalar.activation(sq[:], hub[t][:], ACT.Square)
            nc.scalar.activation(rs[t], sq[:], ACT.Abs_reciprocal_sqrt, bias=1.0)
            nc.scalar.activation(gained[t], hub[t][:], ACT.Copy, scale=gn_t[:, t : t + 1])

        def weave_w2(b):
            cols = slice(b * P, (b + 1) * P)
            nc.scalar.copy(w2g[:, cols, :].rearrange("p (c i) j -> p c j i", i=4), w2raw[:, :, cols].rearrange("p j (c i) -> p c j i", i=4))

        for h in range(2):
            fetch_first(2 * h)
            fetch_first(2 * h + 1)
            add_second(2 * h)
            add_second(2 * h + 1)
            normalise(h)
        normalise(2)
        normalise(3)
        for b in range(N // P):
            weave_w2(b)

        outv = out.rearrange("(b p) c -> p b c", p=P)
        wide = 2 * P
        left = [keep.tile([P, wide], F32, name="left%d" % t) for t in range(PACK)]
        left2 = [keep.tile([P, wide], F32, name="leftb%d" % t) for t in range(PACK)]
        right = [keep.tile([P, wide], F32, name="right%d" % t) for t in range(PACK)]
        zlast = w2buf[:, 2 * S : 3 * S]
        woven01_words = w2buf[:, 2 * S + wide : 3 * S + wide]
        late = keep.tile([P, S], F32, name="late", align_bytes=64)
        woven3 = late[:, :wide].bitcast(BF16)
        woven01 = woven01_words.bitcast(BF16)
        woven2 = w2buf[:, 2 * S + 3 * P : 2 * S + 5 * P].bitcast(BF16)
        zt = [psum.tile([P, PACK, P], F32, name="zt%d" % jb, tag="bank", bufs=8) for jb in range(2)]

        def fetch(dst, t, lst, lo, hi):
            nc.vector.tensor_copy(dst[:], hn[t][:].indirect(lst[:, lo // 16 : hi // 16]))

        def second(z, jb, t):
            lc = slice(jb * P // 16, (jb + 1) * P // 16)
            nc.vector.tensor_tensor(z[:, t * P : (t + 1) * P], hn[t][:].indirect(i2_t[:, lc]), right[t][:, (jb - 2) * P : (jb - 1) * P], ALU.add)

        def weave(dst, z, copy):
            copy(dst.rearrange("p (c i t) -> p c t i", i=4, t=PACK), z.rearrange("p (t c i) -> p c t i", t=PACK, i=4))

        def quantise(woven, width, name):
            codes = keep.tile([P, width], U32, name="zcodes" + name, align_bytes=64)
            scales = keep.tile([P, width], U8, name="zscales" + name, align_bytes=64)
            nc.vector.quantize_mx(out=codes[:].bitcast(FP8X4), scales=scales[:], in_=woven)
            return codes, scales

        def finish(lo, width, codes, scales, per_bank, queues, staged=None):
            cols = slice(lo, lo + width)
            for g, queue in enumerate(queues):
                op = psum.tile([P, per_bank, width], F32, name="op%d_%d" % (lo, g), tag="bank", bufs=8)
                for u in range(per_bank):
                    b = g * per_bank + u
                    nc.tensor.matmul_mx(out=op[:, u, :], lhsT=w2c[:, b * P : (b + 1) * P].bitcast(FP8X4), lhsT_scale=w2s[:, b * P : (b + 1) * P],
                                        rhs=codes[:].bitcast(FP8X4), rhs_scale=scales[:], start=True, stop=True)
                blocks = slice(g * per_bank, (g + 1) * per_bank)
                o_sb = staged if staged is not None else keep.tile([P, per_bank, width], F32, name="o%d_%d" % (lo, g))[:]
                nc.vector.tensor_tensor(o_sb, op[:], res_t[:, blocks, cols], ALU.add)
                queue.dma_start(outv[:, blocks, cols], o_sb)

        for t in range(PACK):
            fetch(left[t], t, i1_t, 0, wide)
            fetch(left2[t], t, i2_t, 0, wide)
            for jb in range(2):
                cols = slice(jb * P, (jb + 1) * P)
                nc.tensor.matmul(zt[jb][:, t, :], left[t][:, cols], ident[:], start=True, stop=False, is_transpose=True)
                nc.tensor.matmul(zt[jb][:, t, :], left2[t][:, cols], ident[:], start=False, stop=True, is_transpose=True)
            fetch(right[t], t, i1_t, wide, S)
        for jb in range(2):
            pairs = keep.tile([P, 2, P, 2], BF16, name="pairs%d" % jb)
            nc.scalar.copy(pairs[:], zt[jb][:].rearrange("j (u e) p -> j u p e", e=2))
            words = pairs[:].rearrange("j u p e -> j (u p e)").bitcast(F32)
            back = psum.tile([P, 2, P], F32, name="back%d" % jb, tag="bank", bufs=8)
            for u in range(2):
                nc.tensor.transpose(back[:, u, :], words[:, u * P : (u + 1) * P], ident[:])
            nc.scalar.copy(woven01_words[:, jb * wide : (jb + 1) * wide].rearrange("p (c u) -> p c u", u=2), back[:].rearrange("p u c -> p c u"))
        nc.vector.quantize_mx(out=w2c[:].bitcast(FP8X4), scales=w2s[:], in_=w2g.rearrange("p c j -> p (c j)"))
        for t in range(PACK):
            second(zb, 2, t)
        second(zlast, 3, 0)
        second(zlast, 3, 1)
        q01 = quantise(woven01, wide, "01")
        weave(woven2, zb[:], nc.scalar.copy)
        second(zlast, 3, 2)
        finish(0, wide, *q01, 2, [nc.sync, nc.sync])
        q2 = quantise(woven2, P, "2")
        second(zlast, 3, PACK - 1)
        weave(woven3, zlast, nc.vector.tensor_copy)
        q3 = quantise(woven3, P, "3")
        finish(2 * P, P, *q2, 4, [nc.sync], late[:].rearrange("p (b c) -> p b c", c=P))
        finish(3 * P, P, *q3, 2, [nc.sync, nc.scalar])
